import numpy as np
import ml_dtypes

BF16 = ml_dtypes.bfloat16


def bf(x):
    return np.asarray(x, np.float32).astype(BF16)


def f32(x):
    return np.asarray(x, np.float32)


def f64(x):
    return np.asarray(x).astype(np.float64)


def striped(idx):
    return np.tile(idx.reshape(-1, 16).T, (8, 1))


def rows(idx, k):
    return np.tile(idx, (k, 1))


def look(tab, idx):
    return np.take_along_axis(f64(tab), rows(idx, len(tab)), axis=1)


K, S, V, N = 256, 2048, 1024, 1024


def setup_inputs():
    return {"tab": f32(np.random.standard_normal((2, K, S))), "y": f32(np.random.standard_normal((K, V))), "offs": striped(np.random.permutation(S)[:N])}


def reference(tab, y, offs):
    idx = offs[:16].T.reshape(-1)
    x = (np.maximum(look(tab[0], idx), f64(y))) * (1.0 / (1.0 + np.exp(-look(tab[1], idx))))
    return x

@@ -1,0 +1,48 @@
+import concourse.mybir as mybir
+
+F32 = mybir.dt.float32
+U16 = mybir.dt.uint16
+MAX = mybir.AluOpType.max
+MULT = mybir.AluOpType.mult
+SIGMOID = mybir.ActivationFunctionType.Sigmoid
+
+P = 128
+STRIPE = 16
+PIECE = 512
+
+
+def tile_lookup_vg_maxsig_out_kernel(tc, tab, y, offs, out):
+    nc = tc.nc
+    n_rows, n_places = tab.shape[1], tab.shape[2]
+    n_entries = y.shape[1]
+    n_blocks = n_rows // P
+
+    with (
+        tc.tile_pool(name="held", bufs=1) as held,
+        tc.tile_pool(name="blocks", bufs=n_blocks) as blocks,
+    ):
+        offsets = held.tile([P, n_entries // STRIPE], U16)
+        nc.sync.dma_start(offsets[:], offs)
+
+        loaded = []
+        for b in range(n_blocks):
+            rows = slice(b * P, (b + 1) * P)
+            values = blocks.tile([P, n_places], F32)
+            stream = blocks.tile([P, n_entries], F32)
+            gates = blocks.tile([P, n_places], F32)
+            nc.sync.dma_start(values[:], tab[0, rows, :])
+            nc.sync.dma_start(stream[:], y[rows, :])
+            nc.sync.dma_start(gates[:], tab[1, rows, :])
+            loaded.append((rows, values, stream, gates))
+
+        for rows, values, stream, gates in loaded:
+            larger = blocks.tile([P, n_entries], F32)
+            opened = blocks.tile([P, n_entries], F32)
+            product = blocks.tile([P, n_entries], F32)
+            for start in range(0, n_entries, PIECE):
+                entries = slice(start, start + PIECE)
+                piece = offsets[:, start // STRIPE : (start + PIECE) // STRIPE]
+                nc.vector.tensor_tensor(larger[:, entries], values[:].indirect(piece), stream[:, entries], MAX)
+                nc.scalar.activation(opened[:, entries], gates[:].indirect(piece), SIGMOID)
+                nc.vector.tensor_tensor(product[:, entries], larger[:, entries], opened[:, entries], MULT)
+                nc.sync.dma_start(out[rows, entries], product[:, entries])

@@ -8,41 +8,65 @@ SIGMOID = mybir.ActivationFunctionType.Sigmoid
 
 P = 128
 STRIPE = 16
-PIECE = 512
+PIECE = 256
 
 
 def tile_lookup_vg_maxsig_out_kernel(tc, tab, y, offs, out):
     nc = tc.nc
-    n_rows, n_places = tab.shape[1], tab.shape[2]
+    n_places = tab.shape[2]
     n_entries = y.shape[1]
-    n_blocks = n_rows // P
+    assert tab.shape[1] == 2 * P
+    first, last = slice(0, P), slice(P, 2 * P)
+    half = n_entries // 2
+    starts = range(0, n_entries, PIECE)
 
-    with (
-        tc.tile_pool(name="held", bufs=1) as held,
-        tc.tile_pool(name="blocks", bufs=n_blocks) as blocks,
-    ):
+    with tc.tile_pool(name="held", bufs=1) as held:
         offsets = held.tile([P, n_entries // STRIPE], U16)
+        values = [held.tile([P, n_places], F32, name=f"values{b}") for b in range(2)]
+        gates = [held.tile([P, n_places], F32, name=f"gates{b}") for b in range(2)]
+        larger = [held.tile([P, n_entries], F32, name=f"larger{b}") for b in range(2)]
+        opened = [held.tile([P, n_entries], F32, name=f"opened{b}") for b in range(2)]
+        y_first = held.tile([P, n_entries], F32)
+        y_early = held.tile([P, half], F32)
+        y_late = held.tile([P, half], F32)
+        product_first = held.tile([P, n_entries], F32)
+
         nc.sync.dma_start(offsets[:], offs)
+        nc.sync.dma_start(gates[0][:], tab[1, first, :])
+        nc.sync.dma_start(values[0][:], tab[0, first, :])
+        nc.sync.dma_start(y_first[:], y[first, :])
+        nc.sync.dma_start(values[1][:], tab[0, last, :])
+        nc.sync.dma_start(y_early[:], y[last, half:])
+        nc.sync.dma_start(gates[1][:], tab[1, last, :])
+        nc.sync.dma_start(y_late[:], y[last, :half])
 
-        loaded = []
-        for b in range(n_blocks):
-            rows = slice(b * P, (b + 1) * P)
-            values = blocks.tile([P, n_places], F32)
-            stream = blocks.tile([P, n_entries], F32)
-            gates = blocks.tile([P, n_places], F32)
-            nc.sync.dma_start(values[:], tab[0, rows, :])
-            nc.sync.dma_start(stream[:], y[rows, :])
-            nc.sync.dma_start(gates[:], tab[1, rows, :])
-            loaded.append((rows, values, stream, gates))
+        def piece(tile, start):
+            return tile[:, start : start + PIECE]
 
-        for rows, values, stream, gates in loaded:
-            larger = blocks.tile([P, n_entries], F32)
-            opened = blocks.tile([P, n_entries], F32)
-            product = blocks.tile([P, n_entries], F32)
-            for start in range(0, n_entries, PIECE):
-                entries = slice(start, start + PIECE)
-                piece = offsets[:, start // STRIPE : (start + PIECE) // STRIPE]
-                nc.vector.tensor_tensor(larger[:, entries], values[:].indirect(piece), stream[:, entries], MAX)
-                nc.scalar.activation(opened[:, entries], gates[:].indirect(piece), SIGMOID)
-                nc.vector.tensor_tensor(product[:, entries], larger[:, entries], opened[:, entries], MULT)
-                nc.sync.dma_start(out[rows, entries], product[:, entries])
+        def listed(start):
+            return offsets[:, start // STRIPE : (start + PIECE) // STRIPE]
+
+        def take_maximum(b, start, y_piece):
+            nc.vector.tensor_tensor(piece(larger[b], start), values[b][:].indirect(listed(start)), y_piece, MAX)
+
+        def open_gate(b, start):
+            nc.scalar.activation(piece(opened[b], start), gates[b][:].indirect(listed(start)), SIGMOID)
+
+        def multiply(b, start, product):
+            nc.vector.tensor_tensor(product, piece(larger[b], start), piece(opened[b], start), MULT)
+
+        for start in starts:
+            open_gate(0, start)
+            take_maximum(0, start, piece(y_first, start))
+            multiply(0, start, piece(product_first, start))
+        nc.sync.dma_start(out[first, :], product_first[:])
+
+        for start in range(0, half, PIECE):
+            take_maximum(1, half + start, piece(y_early, start))
+        for start in range(0, half, PIECE):
+            take_maximum(1, start, piece(y_late, start))
+        for start in starts:
+            product = piece(y_early, start) if start < half else piece(y_late, start - half)
+            open_gate(1, start)
+            multiply(1, start, product)
+            nc.sync.dma_start(out[last, start : start + PIECE], product)

@@ -31,8 +31,8 @@ def tile_lookup_vg_maxsig_out_kernel(tc, tab, y, offs, out):
         y_late = held.tile([P, half], F32)
         product_first = held.tile([P, n_entries], F32)
 
-        nc.sync.dma_start(offsets[:], offs)
         nc.sync.dma_start(gates[0][:], tab[1, first, :])
+        nc.sync.dma_start(offsets[:], offs)
         nc.sync.dma_start(values[0][:], tab[0, first, :])
         nc.sync.dma_start(y_first[:], y[first, :])
         nc.sync.dma_start(values[1][:], tab[0, last, :])

@@ -8,7 +8,12 @@ SIGMOID = mybir.ActivationFunctionType.Sigmoid
 
 P = 128
 STRIPE = 16
-PIECE = 256
+WIDE = 512
+NARROW = 256
+
+
+def cut(start, stop, width):
+    return [slice(k, k + width) for k in range(start, stop, width)]
 
 
 def tile_lookup_vg_maxsig_out_kernel(tc, tab, y, offs, out):
@@ -18,7 +23,6 @@ def tile_lookup_vg_maxsig_out_kernel(tc, tab, y, offs, out):
     assert tab.shape[1] == 2 * P
     first, last = slice(0, P), slice(P, 2 * P)
     half = n_entries // 2
-    starts = range(0, n_entries, PIECE)
 
     with tc.tile_pool(name="held", bufs=1) as held:
         offsets = held.tile([P, n_entries // STRIPE], U16)
@@ -40,33 +44,29 @@ def tile_lookup_vg_maxsig_out_kernel(tc, tab, y, offs, out):
         nc.sync.dma_start(gates[1][:], tab[1, last, :])
         nc.sync.dma_start(y_late[:], y[last, :half])
 
-        def piece(tile, start):
-            return tile[:, start : start + PIECE]
+        def listed(entries):
+            return offsets[:, entries.start // STRIPE : entries.stop // STRIPE]
 
-        def listed(start):
-            return offsets[:, start // STRIPE : (start + PIECE) // STRIPE]
+        def take_maximum(b, entries, y_piece):
+            nc.vector.tensor_tensor(larger[b][:, entries], values[b][:].indirect(listed(entries)), y_piece, MAX)
 
-        def take_maximum(b, start, y_piece):
-            nc.vector.tensor_tensor(piece(larger[b], start), values[b][:].indirect(listed(start)), y_piece, MAX)
+        def open_gate(b, entries):
+            nc.scalar.activation(opened[b][:, entries], gates[b][:].indirect(listed(entries)), SIGMOID)
 
-        def open_gate(b, start):
-            nc.scalar.activation(piece(opened[b], start), gates[b][:].indirect(listed(start)), SIGMOID)
+        def multiply(b, entries, product):
+            nc.vector.tensor_tensor(product, larger[b][:, entries], opened[b][:, entries], MULT)
 
-        def multiply(b, start, product):
-            nc.vector.tensor_tensor(product, piece(larger[b], start), piece(opened[b], start), MULT)
-
-        for start in starts:
-            open_gate(0, start)
-            take_maximum(0, start, piece(y_first, start))
-            multiply(0, start, piece(product_first, start))
+        for entries in cut(0, n_entries, WIDE):
+            open_gate(0, entries)
+            take_maximum(0, entries, y_first[:, entries])
+            multiply(0, entries, product_first[:, entries])
         nc.sync.dma_start(out[first, :], product_first[:])
 
-        for start in range(0, half, PIECE):
-            take_maximum(1, half + start, piece(y_early, start))
-        for start in range(0, half, PIECE):
-            take_maximum(1, start, piece(y_late, start))
-        for start in starts:
-            product = piece(y_early, start) if start < half else piece(y_late, start - half)
-            open_gate(1, start)
-            multiply(1, start, product)
-            nc.sync.dma_start(out[last, start : start + PIECE], product)
+        take_maximum(1, slice(half, n_entries), y_early[:])
+        for entries in cut(0, half, NARROW):
+            take_maximum(1, entries, y_late[:, entries])
+        for start, other_half in ((0, y_early), (half, y_late)):
+            for entries, columns in zip(cut(start, start + half, NARROW), cut(0, half, NARROW)):
+                open_gate(1, entries)
+                multiply(1, entries, other_half[:, columns])
+                nc.sync.dma_start(out[last, entries], other_half[:, columns])

import concourse.mybir as mybir

F32 = mybir.dt.float32
U16 = mybir.dt.uint16
MAX = mybir.AluOpType.max
MULT = mybir.AluOpType.mult
SIGMOID = mybir.ActivationFunctionType.Sigmoid

P = 128
STRIPE = 16
WIDE = 512
NARROW = 256


def cut(start, stop, width):
    return [slice(k, k + width) for k in range(start, stop, width)]


def tile_lookup_vg_maxsig_out_kernel(tc, tab, y, offs, out):
    nc = tc.nc
    n_places = tab.shape[2]
    n_entries = y.shape[1]
    assert tab.shape[1] == 2 * P
    first, last = slice(0, P), slice(P, 2 * P)
    half = n_entries // 2

    with tc.tile_pool(name="held", bufs=1) as held:
        offsets = held.tile([P, n_entries // STRIPE], U16)
        values = [held.tile([P, n_places], F32, name=f"values{b}") for b in range(2)]
        gates = [held.tile([P, n_places], F32, name=f"gates{b}") for b in range(2)]
        larger = [held.tile([P, n_entries], F32, name=f"larger{b}") for b in range(2)]
        opened = [held.tile([P, n_entries], F32, name=f"opened{b}") for b in range(2)]
        y_first = held.tile([P, n_entries], F32)
        y_early = held.tile([P, half], F32)
        y_late = held.tile([P, half], F32)
        product_first = held.tile([P, n_entries], F32)

        nc.sync.dma_start(gates[0][:], tab[1, first, :])
        nc.sync.dma_start(offsets[:], offs)
        nc.sync.dma_start(values[0][:], tab[0, first, :])
        nc.sync.dma_start(y_first[:], y[first, :])
        nc.sync.dma_start(values[1][:], tab[0, last, :])
        nc.sync.dma_start(y_early[:], y[last, half:])
        nc.sync.dma_start(gates[1][:], tab[1, last, :])
        nc.sync.dma_start(y_late[:], y[last, :half])

        def listed(entries):
            return offsets[:, entries.start // STRIPE : entries.stop // STRIPE]

        def take_maximum(b, entries, y_piece):
            nc.vector.tensor_tensor(larger[b][:, entries], values[b][:].indirect(listed(entries)), y_piece, MAX)

        def open_gate(b, entries):
            nc.scalar.activation(opened[b][:, entries], gates[b][:].indirect(listed(entries)), SIGMOID)

        def multiply(b, entries, product):
            nc.vector.tensor_tensor(product, larger[b][:, entries], opened[b][:, entries], MULT)

        for entries in cut(0, n_entries, WIDE):
            open_gate(0, entries)
            take_maximum(0, entries, y_first[:, entries])
            multiply(0, entries, product_first[:, entries])
        nc.sync.dma_start(out[first, :], product_first[:])

        take_maximum(1, slice(half, n_entries), y_early[:])
        for entries in cut(0, half, NARROW):
            take_maximum(1, entries, y_late[:, entries])
        for start, other_half in ((0, y_early), (half, y_late)):
            for entries, columns in zip(cut(start, start + half, NARROW), cut(0, half, NARROW)):
                open_gate(1, entries)
                multiply(1, entries, other_half[:, columns])
                nc.sync.dma_start(out[last, entries], other_half[:, columns])
